import numpy as np
import ml_dtypes


def mxq(x, axis, fmt="e4m3"):
    dtype, down = {"e4m3": (ml_dtypes.float8_e4m3fn, 7), "e5m2": (ml_dtypes.float8_e5m2, 14)}[fmt]
    v = np.moveaxis(np.asarray(x, np.float32).astype(ml_dtypes.bfloat16).astype(np.float64), axis, -1)
    blocks = v.reshape(v.shape[:-1] + (-1, 32))
    amax = np.abs(blocks).max(-1, keepdims=True)
    byte = np.maximum(np.where(amax > 0, np.frexp(amax)[1] - 1 + 127, 0) - down, 1)
    scale = np.exp2(byte - 127.0)
    codes = (blocks / scale).astype(np.float32).astype(dtype).astype(np.float64)
    return np.moveaxis((codes * scale).reshape(v.shape), -1, axis)


WIDE = False


def mx_kscale(k):
    if not WIDE:
        return np.ones(k)
    levels = np.array([10, -10, 5, -5, 0])
    if k % 512:
        return np.exp2(np.random.permutation(np.resize(levels, k // 32))).repeat(32)
    a = np.empty((k // 512, 16))
    for p in range(k // 512):
        a[p, :8] = np.random.permutation(np.resize(levels, 8))
        for g in range(8):
            far = levels[np.abs(levels - a[p, g]) >= 10]
            a[p, g + 8] = far[np.random.randint(len(far))]
    return np.exp2(a.ravel()).repeat(32)


def f64(x):
    return np.asarray(x).astype(np.float64)


def striped(idx):
    return np.tile(idx.reshape(-1, 16).T, (8, 1)).astype(np.uint16)


def unstriped(offs):
    return offs[:16].T.reshape(-1).astype(np.int64)


def pack_weight(w):
    k, n = w.shape
    w = f64(np.asarray(w, np.float32).astype(ml_dtypes.bfloat16)).reshape(k // 32, 32, n)
    amax = np.abs(w).max(1)
    byte = np.clip(np.where(amax > 0, np.frexp(amax)[1] - 1 + 127 - 7, 1), 1, 254)
    scaled = (w * np.exp2(127.0 - byte)[:, None, :]).reshape(k, n).astype(np.float32)
    words = np.ascontiguousarray(scaled.reshape(k // 512, 128, 4, n).transpose(0, 1, 3, 2)).astype(ml_dtypes.float8_e4m3fn).view(np.uint8)
    return words, np.ascontiguousarray(byte.astype(np.uint8).reshape(k // 512, 16, n))


def unpack_weight(words, scales):
    g, p, n, _ = words.shape
    vals = np.ascontiguousarray(words).view(ml_dtypes.float8_e4m3fn).astype(np.float64) * np.repeat(np.exp2(scales.astype(np.float64) - 127.0), 8, axis=1)[..., None]
    return vals.transpose(0, 1, 3, 2).reshape(g * 512, n)


E2M1 = np.array([0.0, 0.5, 1.0, 1.5, 2.0, 3.0, 4.0, 6.0, -0.0, -0.5, -1.0, -1.5, -2.0, -3.0, -4.0, -6.0])


def pack_fp4(w):
    k, n = w.shape
    w = f64(np.asarray(w, np.float32).astype(ml_dtypes.bfloat16)).reshape(k // 32, 32, n)
    amax = np.abs(w).max(1)
    mant, ex = np.frexp(amax / 6.0)
    byte = np.clip(np.where(amax > 0, np.where(mant > 0.5, ex, ex - 1) + 127, 1), 1, 254)
    scaled = (w * np.exp2(127.0 - byte)[:, None, :]).reshape(k, n).astype(np.float32)
    c = np.ascontiguousarray(scaled.reshape(k // 512, 128, 4, n).transpose(0, 1, 3, 2)).astype(ml_dtypes.float4_e2m1fn).view(np.uint8) & 0xF
    words = (c[..., 0::2] | (c[..., 1::2] << 4)).reshape(k // 512, 128, 2 * n)
    return np.ascontiguousarray(words), np.ascontiguousarray(byte.astype(np.uint8).reshape(k // 512, 16, n))


def unpack_fp4(words, scales):
    g, _, n = scales.shape
    words = np.ascontiguousarray(words).reshape(g, 128, n, 2)
    nib = np.empty((g, 128, n, 4), np.uint8)
    nib[..., 0::2] = words & 0xF
    nib[..., 1::2] = words >> 4
    vals = E2M1[nib] * np.repeat(np.exp2(scales.astype(np.float64) - 127.0), 8, axis=1)[..., None]
    return vals.transpose(0, 1, 3, 2).reshape(g * 512, n)


def sigmoid(v):
    return 1.0 / (1.0 + np.exp(-np.maximum(v, -700.0)))


K, T, S, D, N, H, V, U = 512, 4096, 1024, 4, 256, 512, 256, 512


def setup_inputs():
    n = np.random.standard_normal
    s = mx_kscale(K)[:, None]
    u = mx_kscale(H)
    packed_xT = pack_weight(n((K, T)) * s)
    packed_w1 = pack_fp4(n((K, H)) / np.sqrt(K) / s)
    packed_w2 = pack_fp4(n((K, H)) / np.sqrt(K) / s)
    packed_w3 = pack_fp4(n((H, N)) / np.sqrt(H) / u[:, None])
    return {
        "x_words": packed_xT[0],
        "x_scales": packed_xT[1],
        "w1_words": packed_w1[0],
        "w1_scales": packed_w1[1],
        "w2_words": packed_w2[0],
        "w2_scales": packed_w2[1],
        "unit": (np.random.uniform(0.6, 1.4, (H, 1)) * u[:, None]).astype(np.float32),
        "w3_words": packed_w3[0],
        "w3_scales": packed_w3[1],
        "offs": striped(np.random.permutation(T)[:S]),
        "chd": striped(np.random.permutation(S)),
        "wl": striped(np.random.permutation(np.concatenate([np.arange(V), np.random.randint(0, V, U - V)]))),
    }


def reference(x_words, x_scales, w1_words, w1_scales, w2_words, w2_scales, unit, w3_words, w3_scales, offs, chd, wl):
    xq = unpack_weight(x_words, x_scales)[:, unstriped(offs)]
    cs = unpack_fp4(w1_words, w1_scales).T @ xq
    cost = np.log(np.exp(cs) + 1.0)
    cc2_ = cost[:, unstriped(chd)]
    se = unpack_fp4(w2_words, w2_scales).T @ xq
    selv = sigmoid(se)
    inp = cc2_ * selv
    sc_ = selv[:, unstriped(chd)]
    nloop = inp * (sc_ + 0.3) + 0.4 * cost
    hash_ = inp + cost
    best = np.minimum(1.6 * nloop, hash_)
    plan = best.reshape(len(best), -1, D).sum(axis=2)
    tw = plan[:, unstriped(wl)]
    mxc = cost.reshape(len(cost), -1, D).max(axis=2)
    mw = mxc[:, unstriped(wl)]
    hid = f64(unit) * (tw / (mw + 0.5))
    return unpack_fp4(w3_words, w3_scales).T @ mxq(hid, 0, "e4m3")

@@ -1,0 +1,258 @@
+from contextlib import ExitStack
+
+import concourse.mybir as mybir
+from concourse.masks import make_identity
+
+K, T, S, D, N, H, V, U = 512, 4096, 1024, 4, 256, 512, 256, 512
+FLOPS = 2 * K * H * S * 2 + 2 * H * N * U
+
+F32 = mybir.dt.float32
+BF16 = mybir.dt.bfloat16
+I32 = mybir.dt.int32
+U32 = mybir.dt.uint32
+U16 = mybir.dt.uint16
+U8 = mybir.dt.uint8
+FP8X4 = mybir.dt.float8_e4m3fn_x4
+FP4X4 = mybir.dt.float4_e2m1fn_x4
+ACT = mybir.ActivationFunctionType
+ALU = mybir.AluOpType
+
+P = 128
+TILES = H // P
+HALF = S // 2
+VH = V // 2
+UH = U // 2
+EXP_CAP = 2.0**60
+
+
+def tile_picked_ydbtune_rel_p_kernel(
+    tc, x_words, x_scales, w1_words, w1_scales, w2_words, w2_scales, unit, w3_words, w3_scales, offs, chd, wl, out
+):
+    nc = tc.nc
+    with ExitStack() as ctx:
+        keep = ctx.enter_context(tc.tile_pool(name="keep", bufs=1))
+        ring = ctx.enter_context(tc.tile_pool(name="ring", bufs=2))
+        psum = ctx.enter_context(tc.psum_pool(name="psum", bufs=1))
+
+        def bank(t, h, cols, name):
+            return psum.tile([P, cols], F32, tag=f"bank{2 * t + h}", name=name)
+
+        def half(h):
+            return slice(h * HALF, (h + 1) * HALF)
+
+        def load_scale_rows(queue, dst, src):
+            for q in range(4):
+                queue.dma_start(out=dst[32 * q : 32 * q + 4, :].bitcast(I32), in_=src[0, 4 * q : 4 * q + 4, :].bitcast(I32))
+
+        offs_sb = keep.tile([P, S // 16], U16, name="offs_sb")
+        chd_sb = keep.tile([P, S // 16], U16, name="chd_sb")
+        wl_sb = keep.tile([P, U // 16], U16, name="wl_sb")
+        x_table = keep.tile([P, T], U32, name="x_table", align_bytes=64)
+        xs_table = keep.tile([P, T], U8, name="xs_table", align_bytes=64)
+        w_raw = keep.tile([P, 2 * H], U8, name="w_raw", align_bytes=64)
+        ws_raw = keep.tile([P, H], U8, name="ws_raw", align_bytes=64)
+        unit_sb = keep.tile([P, TILES], F32, name="unit_sb")
+        tanh_w = [keep.tile([P, 2 * S], F32, name=f"tanh_w{t}") for t in range(TILES)]
+
+        nc.vector.memset(xs_table[:].bitcast(I32), 0)
+        nc.gpsimd.memset(ws_raw[:].bitcast(I32), 0)
+
+        nc.sync.dma_start(offs_sb[:], offs)
+        nc.sync.dma_start(out=x_table[:].bitcast(I32), in_=x_words[0].rearrange("p n t -> p (n t)").bitcast(I32))
+        nc.scalar.dma_start(out=w_raw[:].bitcast(I32), in_=w2_words[0].bitcast(I32))
+        load_scale_rows(nc.scalar, xs_table, x_scales)
+        load_scale_rows(nc.gpsimd, ws_raw, w2_scales)
+        nc.gpsimd.dma_start(out=unit_sb[:], in_=unit.rearrange("(p t) o -> p (t o)", t=TILES))
+        nc.sync.dma_start(chd_sb[:], chd)
+        nc.sync.dma_start(wl_sb[:], wl)
+
+        for t in range(2):
+            nc.vector.memset(tanh_w[t][:, S:], 0.0)
+        ident = keep.tile([P, P], F32, name="ident")
+        make_identity(nc, ident[:])
+
+        unit64 = keep.tile([P, TILES], F32, name="unit64")
+        nc.scalar.activation(unit64[:], unit_sb[:], ACT.Copy, scale=0.64)
+
+        w_dealt = [keep.tile([P, 2 * H], U8, name=f"w_dealt{i}", align_bytes=64) for i in range(2)]
+        ws_dealt = [keep.tile([P, H], U8, name=f"ws_dealt{i}", align_bytes=64) for i in range(2)]
+
+        def deal(i):
+            nc.vector.tensor_copy(
+                w_dealt[i][:].rearrange("p (t m b) -> p t m b", t=TILES, b=2),
+                w_raw[:].rearrange("p (m t b) -> p t m b", t=TILES, b=2),
+            )
+            nc.vector.tensor_copy(
+                ws_dealt[i][:].rearrange("p (t m) -> p t m", t=TILES),
+                ws_raw[:].rearrange("p (m t) -> p t m", t=TILES),
+            )
+
+        xq_scales = keep.tile([P, S], U8, name="xq_scales", align_bytes=64)
+        xq_words = [keep.tile([P, HALF], U32, name=f"xq_words{h}", align_bytes=64) for h in range(2)]
+        nc.vector.tensor_copy(xq_scales[:], xs_table[:].indirect(offs_sb[:]))
+        deal(0)
+        nc.sync.dma_start(out=w_raw[:].bitcast(I32), in_=w1_words[0].bitcast(I32))
+        load_scale_rows(nc.sync, ws_raw, w1_scales)
+        for h in range(2):
+            nc.vector.tensor_copy(xq_words[h][:], x_table[:].indirect(offs_sb[:, h * HALF // 16 : (h + 1) * HALF // 16]))
+        deal(1)
+        nc.sync.dma_start(out=w_raw[:, : 2 * N].bitcast(I32), in_=w3_words[0].bitcast(I32))
+        load_scale_rows(nc.sync, ws_raw[:, :N], w3_scales)
+
+        def product(i, t, h, name):
+            acc = bank(t, h, HALF, name)
+            nc.tensor.matmul_mx(
+                out=acc[:],
+                lhsT=w_dealt[i][:, 2 * P * t : 2 * P * (t + 1)].bitcast(FP4X4),
+                lhsT_scale=ws_dealt[i][:, P * t : P * (t + 1)],
+                rhs=xq_words[h][:].bitcast(FP8X4),
+                rhs_scale=xq_scales[:, half(h)],
+                start=True,
+                stop=True,
+            )
+            return acc
+
+        def chd_half(h):
+            return chd_sb[:, h * HALF // 16 : (h + 1) * HALF // 16]
+
+        for t in range(TILES):
+            for h in range(2):
+                se = product(0, t, h, f"se{t}{h}")
+                nc.scalar.activation(tanh_w[t][:, half(h)], se[:], ACT.Tanh, scale=0.5)
+
+        slope = [tanh_w[2][:, S:], tanh_w[3][:, S:]] + [keep.tile([P, S], F32, name=f"slope{t}")[:] for t in (2, 3)]
+
+        def gather_slope(t):
+            for h in range(2):
+                nc.vector.tensor_scalar(slope[t][:, half(h)], tanh_w[t][:].indirect(chd_half(h)), 0.8, 0.28, ALU.mult, ALU.add)
+
+        gather_slope(0)
+        gather_slope(1)
+        cs = {}
+        expo = [keep.tile([P, S], F32, name=f"expo{t}") for t in range(TILES)]
+        for t in range(TILES):
+            for h in range(2):
+                cs[t, h] = product(1, t, h, f"cs{t}{h}")
+                nc.scalar.activation(expo[t][:, half(h)], cs[t, h][:], ACT.Exp)
+            nc.vector.tensor_scalar(expo[t][:], expo[t][:], EXP_CAP, None, ALU.min)
+            if t in (0, 2):
+                gather_slope(2 + t // 2)
+
+        cost = [keep.tile([P, S], F32, name=f"cost{t}") for t in range(TILES)]
+        ratio_w = [keep.tile([P, S], F32, name=f"ratio_w{t}") for t in range(TILES)]
+        log_den = keep.tile([P, TILES * V], F32, name="log_den")
+        inv_den = keep.tile([P, TILES * V], F32, name="inv_den")
+        sums = {}
+
+        def add_groups(t, h, src_of_d, first, last):
+            for d in range(D):
+                nc.tensor.matmul(sums[t, h][:], src_of_d(d), ident[:], is_transpose=True, start=first and d == 0, stop=last and d == D - 1)
+
+        def softplus(t):
+            soft = ring.tile([P, S], F32, name="soft")
+            nc.scalar.activation(soft[:], expo[t][:], ACT.Ln, bias=1.0)
+            for h in range(2):
+                nc.vector.tensor_tensor(cost[t][:, half(h)], cs[t, h][:], soft[:, half(h)], ALU.max)
+            for h in range(2):
+                sums[t, h] = bank(t, h, P, f"sums{t}{h}")
+                add_groups(t, h, lambda d: cost[t][:, h * HALF + d : (h + 1) * HALF : D], True, False)
+
+        def largest(ts):
+            for t in ts:
+                quad = cost[t][:].rearrange("p (v d) -> p v d", d=D)
+                nc.vector.tensor_tensor(ratio_w[t][:, 2 * V :].rearrange("p (v e) -> p v e", e=2), quad[:, :, 0:2], quad[:, :, 2:4], ALU.max)
+            for t in ts:
+                nc.vector.tensor_tensor(ratio_w[t][:, V : 2 * V], ratio_w[t][:, 2 * V :: 2], ratio_w[t][:, 2 * V + 1 :: 2], ALU.max)
+
+        child = {}
+
+        def gather_child(t):
+            child[t] = ring.tile([P, S], F32, name="child")
+            for h in range(2):
+                nc.scalar.activation(child[t][:, half(h)], cost[t][:].indirect(chd_half(h)), ACT.Copy, scale=0.5 / 0.64)
+
+        softplus(0)
+        softplus(1)
+        largest((0, 1))
+        softplus(2)
+        softplus(3)
+        largest((2, 3))
+        gather_child(0)
+        gather_child(1)
+        for t in range(TILES):
+            nc.scalar.activation(log_den[:, V * t : V * (t + 1)], ratio_w[t][:, V : 2 * V], ACT.Ln, bias=0.5)
+        nc.scalar.activation(inv_den[:], log_den[:], ACT.Exp, scale=-1.0)
+
+        planes = [keep.tile([P, TILES, UH], BF16, name=f"planes{u}") for u in range(2)]
+
+        def join_costs(t):
+            inp = ring.tile([P, S], F32, name="inp")
+            gain = ring.tile([P, S], F32, name="gain")
+            low = ring.tile([P, 2, D, VH], F32, name="low")
+            for h in range(2):
+                nc.vector.scalar_tensor_tensor(inp[:, half(h)], tanh_w[t][:, half(h)], 1.0, child[t][:, half(h)], ALU.add, ALU.mult)
+            for h in range(2):
+                nc.vector.tensor_tensor(gain[:, half(h)], inp[:, half(h)], slope[t][:, half(h)], ALU.mult)
+                add_groups(t, h, lambda d: inp[:, h * HALF + d : (h + 1) * HALF : D], False, False)
+            for h in range(2):
+                nc.vector.scalar_tensor_tensor(
+                    low[:, h].rearrange("p d v -> p v d"),
+                    cost[t][:, half(h)].rearrange("p (v d) -> p v d", d=D),
+                    0.36 / 0.64,
+                    gain[:, half(h)].rearrange("p (v d) -> p v d", d=D),
+                    ALU.mult,
+                    ALU.min,
+                )
+                add_groups(t, h, lambda d: low[:, h, d, :], False, True)
+
+        def finish(t):
+            for h in range(2):
+                turned = ring.tile([P, P], F32, name="turned")
+                nc.scalar.copy(turned[:], sums[t, h][:])
+                plan = bank(t, h, P, f"plan{t}{h}")
+                nc.tensor.transpose(plan[:], turned[:], ident[:])
+                nc.vector.scalar_tensor_tensor(
+                    ratio_w[t][:, h * VH : (h + 1) * VH],
+                    plan[:],
+                    unit64[:, t : t + 1],
+                    inv_den[:, V * t + h * VH : V * t + (h + 1) * VH],
+                    ALU.mult,
+                    ALU.mult,
+                )
+            for u in range(2):
+                nc.scalar.activation(planes[u][:, t, :], ratio_w[t][:].indirect(wl_sb[:, u * UH // 16 : (u + 1) * UH // 16]), ACT.Copy)
+
+        for t in range(TILES):
+            if t >= 2:
+                gather_child(t)
+            join_costs(t)
+            if t >= 1:
+                finish(t - 1)
+        finish(TILES - 1)
+
+        for u in range(2):
+            hid = ring.tile([P, UH, TILES], BF16, name="hid", align_bytes=64)
+            nc.vector.tensor_copy(
+                hid[:].rearrange("p (c i) t -> p c t i", i=4),
+                planes[u][:].rearrange("p t (c i) -> p c t i", i=4),
+            )
+            hid_words = ring.tile([P, UH], U32, name="hid_words", align_bytes=64)
+            hid_scales = ring.tile([P, UH], U8, name="hid_scales", align_bytes=64)
+            nc.vector.quantize_mx(out=hid_words[:].bitcast(FP8X4), scales=hid_scales[:], in_=hid[:].rearrange("p c t -> p (c t)"))
+            for mb in range(N // P):
+                acc = bank(u, mb, UH, f"knobs{u}{mb}")
+                nc.tensor.matmul_mx(
+                    out=acc[:],
+                    lhsT=w_raw[:, 2 * P * mb : 2 * P * (mb + 1)].bitcast(FP4X4),
+                    lhsT_scale=ws_raw[:, P * mb : P * (mb + 1)],
+                    rhs=hid_words[:].bitcast(FP8X4),
+                    rhs_scale=hid_scales[:],
+                    start=True,
+                    stop=True,
+                )
+                result = keep.tile([P, UH], F32, name=f"result{u}{mb}")
+                if mb == 0:
+                    nc.scalar.copy(result[:], acc[:])
+                else:
+                    nc.vector.tensor_copy(result[:], acc[:])
+                nc.sync.dma_start(out=out[P * mb : P * (mb + 1), u * UH : (u + 1) * UH], in_=result[:])

@@ -22,7 +22,7 @@ TILES = H // P
 HALF = S // 2
 VH = V // 2
 UH = U // 2
-EXP_CAP = 2.0**60
+LN_CAP = 44.0
 
 
 def tile_picked_ydbtune_rel_p_kernel(
@@ -31,6 +31,7 @@ def tile_picked_ydbtune_rel_p_kernel(
     nc = tc.nc
     with ExitStack() as ctx:
         keep = ctx.enter_context(tc.tile_pool(name="keep", bufs=1))
+        head = ctx.enter_context(tc.tile_pool(name="head", bufs=1))
         ring = ctx.enter_context(tc.tile_pool(name="ring", bufs=2))
         psum = ctx.enter_context(tc.psum_pool(name="psum", bufs=1))
 
@@ -47,24 +48,31 @@ def tile_picked_ydbtune_rel_p_kernel(
         offs_sb = keep.tile([P, S // 16], U16, name="offs_sb")
         chd_sb = keep.tile([P, S // 16], U16, name="chd_sb")
         wl_sb = keep.tile([P, U // 16], U16, name="wl_sb")
-        x_table = keep.tile([P, T], U32, name="x_table", align_bytes=64)
-        xs_table = keep.tile([P, T], U8, name="xs_table", align_bytes=64)
+        x_table = keep.tile([P, T], U32, name="x_table", tag="x_table", align_bytes=64)
+        xs_table = head.tile([P, T], U8, name="xs_table", align_bytes=64, offset=0)
         w_raw = keep.tile([P, 2 * H], U8, name="w_raw", align_bytes=64)
         ws_raw = keep.tile([P, H], U8, name="ws_raw", align_bytes=64)
         unit_sb = keep.tile([P, TILES], F32, name="unit_sb")
-        tanh_w = [keep.tile([P, 2 * S], F32, name=f"tanh_w{t}") for t in range(TILES)]
+        w1_raw = head.tile([P, 2 * H], U8, name="w1_raw", align_bytes=64, offset=2 * T)
+        w1s_raw = head.tile([P, H], U8, name="w1s_raw", align_bytes=64, offset=2 * T + 2 * H)
+        tanh_w = {t: keep.tile([P, 2 * S], F32, name=f"tanh_w{t}") for t in (0, 1, 3)}
 
         nc.vector.memset(xs_table[:].bitcast(I32), 0)
         nc.gpsimd.memset(ws_raw[:].bitcast(I32), 0)
+        nc.gpsimd.memset(w1s_raw[:].bitcast(I32), 0)
 
+        x_rows = x_words[0].rearrange("p n t -> p (n t)").bitcast(I32)
         nc.sync.dma_start(offs_sb[:], offs)
-        nc.sync.dma_start(out=x_table[:].bitcast(I32), in_=x_words[0].rearrange("p n t -> p (n t)").bitcast(I32))
         nc.scalar.dma_start(out=w_raw[:].bitcast(I32), in_=w2_words[0].bitcast(I32))
-        load_scale_rows(nc.scalar, xs_table, x_scales)
+        nc.sync.dma_start(out=x_table[:, : T // 4].bitcast(I32), in_=x_rows[:, : T // 4])
+        load_scale_rows(nc.sync, xs_table, x_scales)
+        nc.sync.dma_start(out=x_table[:, T // 4 :].bitcast(I32), in_=x_rows[:, T // 4 :])
         load_scale_rows(nc.gpsimd, ws_raw, w2_scales)
         nc.gpsimd.dma_start(out=unit_sb[:], in_=unit.rearrange("(p t) o -> p (t o)", t=TILES))
         nc.sync.dma_start(chd_sb[:], chd)
         nc.sync.dma_start(wl_sb[:], wl)
+        nc.sync.dma_start(out=w1_raw[:].bitcast(I32), in_=w1_words[0].bitcast(I32))
+        load_scale_rows(nc.sync, w1s_raw, w1_scales)
 
         for t in range(2):
             nc.vector.memset(tanh_w[t][:, S:], 0.0)
@@ -74,28 +82,35 @@ def tile_picked_ydbtune_rel_p_kernel(
         unit64 = keep.tile([P, TILES], F32, name="unit64")
         nc.scalar.activation(unit64[:], unit_sb[:], ACT.Copy, scale=0.64)
 
-        w_dealt = [keep.tile([P, 2 * H], U8, name=f"w_dealt{i}", align_bytes=64) for i in range(2)]
-        ws_dealt = [keep.tile([P, H], U8, name=f"ws_dealt{i}", align_bytes=64) for i in range(2)]
+        w_dealt = {}
+        ws_dealt = {}
 
-        def deal(i):
+        def deal(i, words, scales, raw_words, raw_scales):
+            w_dealt[i] = words
+            ws_dealt[i] = scales
             nc.vector.tensor_copy(
-                w_dealt[i][:].rearrange("p (t m b) -> p t m b", t=TILES, b=2),
-                w_raw[:].rearrange("p (m t b) -> p t m b", t=TILES, b=2),
+                words.rearrange("p (t m b) -> p t m b", t=TILES, b=2),
+                raw_words[:].rearrange("p (m t b) -> p t m b", t=TILES, b=2),
             )
             nc.vector.tensor_copy(
-                ws_dealt[i][:].rearrange("p (t m) -> p t m", t=TILES),
-                ws_raw[:].rearrange("p (m t) -> p t m", t=TILES),
+                scales.rearrange("p (t m) -> p t m", t=TILES),
+                raw_scales[:].rearrange("p (m t) -> p t m", t=TILES),
             )
 
         xq_scales = keep.tile([P, S], U8, name="xq_scales", align_bytes=64)
-        xq_words = [keep.tile([P, HALF], U32, name=f"xq_words{h}", align_bytes=64) for h in range(2)]
         nc.vector.tensor_copy(xq_scales[:], xs_table[:].indirect(offs_sb[:]))
-        deal(0)
-        nc.sync.dma_start(out=w_raw[:].bitcast(I32), in_=w1_words[0].bitcast(I32))
-        load_scale_rows(nc.sync, ws_raw, w1_scales)
+        xq_words = [
+            head.tile([P, HALF], U32, name="xq_words0", align_bytes=64, offset=0),
+            head.tile([P, HALF], U32, name="xq_words1", align_bytes=64, offset=4 * HALF + H),
+        ]
+        w2_dealt = keep.tile([P, 2 * H], U8, name="w2_dealt", align_bytes=64)
+        w2s_dealt = head.tile([P, H], U8, name="w2s_dealt", align_bytes=64, offset=4 * HALF)
+        deal(0, w2_dealt[:], w2s_dealt[:], w_raw, ws_raw)
         for h in range(2):
             nc.vector.tensor_copy(xq_words[h][:], x_table[:].indirect(offs_sb[:, h * HALF // 16 : (h + 1) * HALF // 16]))
-        deal(1)
+        w1_dealt = keep.tile([P, 3 * H], U8, name="w1_dealt", tag="x_table", align_bytes=64)
+        deal(1, w1_dealt[:, : 2 * H], w1_dealt[:, 2 * H :], w1_raw, w1s_raw)
+        tanh_w[2] = head.tile([P, 2 * S], F32, name="tanh_w2", align_bytes=64, offset=2 * T)
         nc.sync.dma_start(out=w_raw[:, : 2 * N].bitcast(I32), in_=w3_words[0].bitcast(I32))
         load_scale_rows(nc.sync, ws_raw[:, :N], w3_scales)
 
@@ -129,14 +144,13 @@ def tile_picked_ydbtune_rel_p_kernel(
         gather_slope(0)
         gather_slope(1)
         cs = {}
-        expo = [keep.tile([P, S], F32, name=f"expo{t}") for t in range(TILES)]
+        expo = [keep.tile([P, S], F32, name=f"expo{t}", tag=f"expo{t}") for t in range(TILES)]
         for t in range(TILES):
             for h in range(2):
                 cs[t, h] = product(1, t, h, f"cs{t}{h}")
                 nc.scalar.activation(expo[t][:, half(h)], cs[t, h][:], ACT.Exp)
-            nc.vector.tensor_scalar(expo[t][:], expo[t][:], EXP_CAP, None, ALU.min)
-            if t in (0, 2):
-                gather_slope(2 + t // 2)
+        gather_slope(2)
+        gather_slope(3)
 
         cost = [keep.tile([P, S], F32, name=f"cost{t}") for t in range(TILES)]
         ratio_w = [keep.tile([P, S], F32, name=f"ratio_w{t}") for t in range(TILES)]
@@ -149,10 +163,10 @@ def tile_picked_ydbtune_rel_p_kernel(
                 nc.tensor.matmul(sums[t, h][:], src_of_d(d), ident[:], is_transpose=True, start=first and d == 0, stop=last and d == D - 1)
 
         def softplus(t):
-            soft = ring.tile([P, S], F32, name="soft")
+            soft = keep.tile([P, S], F32, name=f"soft{t}")
             nc.scalar.activation(soft[:], expo[t][:], ACT.Ln, bias=1.0)
             for h in range(2):
-                nc.vector.tensor_tensor(cost[t][:, half(h)], cs[t, h][:], soft[:, half(h)], ALU.max)
+                nc.vector.scalar_tensor_tensor(cost[t][:, half(h)], soft[:, half(h)], LN_CAP, cs[t, h][:], ALU.min, ALU.max)
             for h in range(2):
                 sums[t, h] = bank(t, h, P, f"sums{t}{h}")
                 add_groups(t, h, lambda d: cost[t][:, h * HALF + d : (h + 1) * HALF : D], True, False)
@@ -167,7 +181,7 @@ def tile_picked_ydbtune_rel_p_kernel(
         child = {}
 
         def gather_child(t):
-            child[t] = ring.tile([P, S], F32, name="child")
+            child[t] = keep.tile([P, S], F32, name=f"child{t}", tag=f"expo{t}")
             for h in range(2):
                 nc.scalar.activation(child[t][:, half(h)], cost[t][:].indirect(chd_half(h)), ACT.Copy, scale=0.5 / 0.64)
 
@@ -222,9 +236,9 @@ def tile_picked_ydbtune_rel_p_kernel(
             for u in range(2):
                 nc.scalar.activation(planes[u][:, t, :], ratio_w[t][:].indirect(wl_sb[:, u * UH // 16 : (u + 1) * UH // 16]), ACT.Copy)
 
+        gather_child(2)
+        gather_child(3)
         for t in range(TILES):
-            if t >= 2:
-                gather_child(t)
             join_costs(t)
             if t >= 1:
                 finish(t - 1)
@@ -255,4 +269,4 @@ def tile_picked_ydbtune_rel_p_kernel(
                     nc.scalar.copy(result[:], acc[:])
                 else:
                     nc.vector.tensor_copy(result[:], acc[:])
-                nc.sync.dma_start(out=out[P * mb : P * (mb + 1), u * UH : (u + 1) * UH], in_=result[:])
+                (nc.scalar if mb == 0 else nc.sync).dma_start(out=out[P * mb : P * (mb + 1), u * UH : (u + 1) * UH], in_=result[:])

@@ -21,7 +21,7 @@ P = 128
 TILES = H // P
 HALF = S // 2
 VH = V // 2
-UH = U // 2
+PIECES = ((0, 256), (256, 512))
 LN_CAP = 44.0
 
 
@@ -50,16 +50,17 @@ def tile_picked_ydbtune_rel_p_kernel(
         wl_sb = keep.tile([P, U // 16], U16, name="wl_sb")
         x_table = keep.tile([P, T], U32, name="x_table", tag="x_table", align_bytes=64)
         xs_table = head.tile([P, T], U8, name="xs_table", align_bytes=64, offset=0)
-        w_raw = keep.tile([P, 2 * H], U8, name="w_raw", align_bytes=64)
+        w_raw = keep.tile([P, 2 * H], U8, name="w_raw", tag="w_raw", align_bytes=64)
         ws_raw = keep.tile([P, H], U8, name="ws_raw", align_bytes=64)
         unit_sb = keep.tile([P, TILES], F32, name="unit_sb")
-        w1_raw = head.tile([P, 2 * H], U8, name="w1_raw", align_bytes=64, offset=2 * T)
-        w1s_raw = head.tile([P, H], U8, name="w1s_raw", align_bytes=64, offset=2 * T + 2 * H)
-        tanh_w = {t: keep.tile([P, 2 * S], F32, name=f"tanh_w{t}") for t in (0, 1, 3)}
+        w1_staged = head.tile([P, 3 * H], U8, name="w1_staged", align_bytes=64, offset=4 * T - 2 * H)
+        w1_raw = w1_staged[:, : 2 * H]
+        w1s_raw = w1_staged[:, 2 * H :]
+        tanh_w = {t: keep.tile([P, 2 * S], F32, name=f"tanh_w{t}") for t in (0, 1)}
 
         nc.vector.memset(xs_table[:].bitcast(I32), 0)
         nc.gpsimd.memset(ws_raw[:].bitcast(I32), 0)
-        nc.gpsimd.memset(w1s_raw[:].bitcast(I32), 0)
+        nc.gpsimd.memset(w1s_raw.bitcast(I32), 0)
 
         x_rows = x_words[0].rearrange("p n t -> p (n t)").bitcast(I32)
         nc.sync.dma_start(offs_sb[:], offs)
@@ -71,7 +72,7 @@ def tile_picked_ydbtune_rel_p_kernel(
         nc.gpsimd.dma_start(out=unit_sb[:], in_=unit.rearrange("(p t) o -> p (t o)", t=TILES))
         nc.sync.dma_start(chd_sb[:], chd)
         nc.sync.dma_start(wl_sb[:], wl)
-        nc.sync.dma_start(out=w1_raw[:].bitcast(I32), in_=w1_words[0].bitcast(I32))
+        nc.sync.dma_start(out=w1_raw.bitcast(I32), in_=w1_words[0].bitcast(I32))
         load_scale_rows(nc.sync, w1s_raw, w1_scales)
 
         for t in range(2):
@@ -85,34 +86,38 @@ def tile_picked_ydbtune_rel_p_kernel(
         w_dealt = {}
         ws_dealt = {}
 
-        def deal(i, words, scales, raw_words, raw_scales):
+        def deal_words(i, words, raw):
             w_dealt[i] = words
-            ws_dealt[i] = scales
             nc.vector.tensor_copy(
                 words.rearrange("p (t m b) -> p t m b", t=TILES, b=2),
-                raw_words[:].rearrange("p (m t b) -> p t m b", t=TILES, b=2),
-            )
-            nc.vector.tensor_copy(
-                scales.rearrange("p (t m) -> p t m", t=TILES),
-                raw_scales[:].rearrange("p (m t) -> p t m", t=TILES),
+                raw.rearrange("p (m t b) -> p t m b", t=TILES, b=2),
             )
 
-        xq_scales = keep.tile([P, S], U8, name="xq_scales", align_bytes=64)
+        def deal_scales(i, scales, raw):
+            ws_dealt[i] = scales
+            nc.vector.tensor_copy(
+                scales.rearrange("p (t m) -> p t m", t=TILES),
+                raw.rearrange("p (m t) -> p t m", t=TILES),
+            )
+
+        w2_dealt = keep.tile([P, 2 * H], U8, name="w2_dealt", tag="w2_dealt", align_bytes=64)
+        deal_words(0, w2_dealt[:], w_raw[:])
+        xq_scales = keep.tile([P, S], U8, name="xq_scales", tag="w_raw", align_bytes=64)
         nc.vector.tensor_copy(xq_scales[:], xs_table[:].indirect(offs_sb[:]))
         xq_words = [
             head.tile([P, HALF], U32, name="xq_words0", align_bytes=64, offset=0),
             head.tile([P, HALF], U32, name="xq_words1", align_bytes=64, offset=4 * HALF + H),
         ]
-        w2_dealt = keep.tile([P, 2 * H], U8, name="w2_dealt", align_bytes=64)
         w2s_dealt = head.tile([P, H], U8, name="w2s_dealt", align_bytes=64, offset=4 * HALF)
-        deal(0, w2_dealt[:], w2s_dealt[:], w_raw, ws_raw)
+        deal_scales(0, w2s_dealt[:], ws_raw[:])
+        load_scale_rows(nc.sync, ws_raw[:, :N], w3_scales)
         for h in range(2):
             nc.vector.tensor_copy(xq_words[h][:], x_table[:].indirect(offs_sb[:, h * HALF // 16 : (h + 1) * HALF // 16]))
         w1_dealt = keep.tile([P, 3 * H], U8, name="w1_dealt", tag="x_table", align_bytes=64)
-        deal(1, w1_dealt[:, : 2 * H], w1_dealt[:, 2 * H :], w1_raw, w1s_raw)
+        deal_words(1, w1_dealt[:, : 2 * H], w1_raw)
+        deal_scales(1, w1_dealt[:, 2 * H :], w1s_raw)
         tanh_w[2] = head.tile([P, 2 * S], F32, name="tanh_w2", align_bytes=64, offset=2 * T)
-        nc.sync.dma_start(out=w_raw[:, : 2 * N].bitcast(I32), in_=w3_words[0].bitcast(I32))
-        load_scale_rows(nc.sync, ws_raw[:, :N], w3_scales)
+        tanh_w[3] = head.tile([P, 2 * S], F32, name="tanh_w3", align_bytes=64, offset=4 * T)
 
         def product(i, t, h, name):
             acc = bank(t, h, HALF, name)
@@ -134,6 +139,9 @@ def tile_picked_ydbtune_rel_p_kernel(
             for h in range(2):
                 se = product(0, t, h, f"se{t}{h}")
                 nc.scalar.activation(tanh_w[t][:, half(h)], se[:], ACT.Tanh, scale=0.5)
+
+        w3_sb = keep.tile([P, 2 * N], U8, name="w3_sb", tag="w2_dealt", align_bytes=64)
+        nc.sync.dma_start(out=w3_sb[:].bitcast(I32), in_=w3_words[0].bitcast(I32))
 
         slope = [tanh_w[2][:, S:], tanh_w[3][:, S:]] + [keep.tile([P, S], F32, name=f"slope{t}")[:] for t in (2, 3)]
 
@@ -197,27 +205,39 @@ def tile_picked_ydbtune_rel_p_kernel(
             nc.scalar.activation(log_den[:, V * t : V * (t + 1)], ratio_w[t][:, V : 2 * V], ACT.Ln, bias=0.5)
         nc.scalar.activation(inv_den[:], log_den[:], ACT.Exp, scale=-1.0)
 
-        planes = [keep.tile([P, TILES, UH], BF16, name=f"planes{u}") for u in range(2)]
+        planes = keep.tile([P, TILES - 1, U], BF16, name="planes")
+        last_plane = [keep.tile([P, b - a], BF16, name=f"last_plane{a}") for a, b in PIECES]
+        hid = [keep.tile([P, b - a, TILES], BF16, name=f"hid{a}", align_bytes=64) for a, b in PIECES]
 
         def join_costs(t):
-            inp = ring.tile([P, S], F32, name="inp")
-            gain = ring.tile([P, S], F32, name="gain")
-            low = ring.tile([P, 2, D, VH], F32, name="low")
-            for h in range(2):
-                nc.vector.scalar_tensor_tensor(inp[:, half(h)], tanh_w[t][:, half(h)], 1.0, child[t][:, half(h)], ALU.add, ALU.mult)
-            for h in range(2):
-                nc.vector.tensor_tensor(gain[:, half(h)], inp[:, half(h)], slope[t][:, half(h)], ALU.mult)
-                add_groups(t, h, lambda d: inp[:, h * HALF + d : (h + 1) * HALF : D], False, False)
-            for h in range(2):
-                nc.vector.scalar_tensor_tensor(
-                    low[:, h].rearrange("p d v -> p v d"),
-                    cost[t][:, half(h)].rearrange("p (v d) -> p v d", d=D),
-                    0.36 / 0.64,
-                    gain[:, half(h)].rearrange("p (v d) -> p v d", d=D),
-                    ALU.mult,
-                    ALU.min,
-                )
-                add_groups(t, h, lambda d: low[:, h, d, :], False, True)
+            inp = ring.tile([P, D, V], F32, name="inp")
+            gain = ring.tile([P, 2, HALF], F32, name="gain")
+            low = ring.tile([P, D, V], F32, name="low")
+
+            def pairs(row, a):
+                return row.rearrange("p (v d) -> p v d", d=D)[:, :, 2 * a : 2 * a + 2]
+
+            def packed(plane):
+                return plane.rearrange("p (v b) -> p v b", b=2)
+
+            def split(planes_by_d, a):
+                return planes_by_d[:, 2 * a : 2 * a + 2, :].rearrange("p b v -> p v b")
+
+            def add_pairs(src, a, last):
+                for h in range(2):
+                    for b in range(2):
+                        nc.tensor.matmul(
+                            sums[t, h][:], src[:, 2 * a + b, VH * h : VH * (h + 1)], ident[:], is_transpose=True, start=False, stop=last and b == 1
+                        )
+
+            for a in range(2):
+                nc.vector.scalar_tensor_tensor(split(inp, a), pairs(tanh_w[t][:, :S], a), 1.0, pairs(child[t][:], a), ALU.add, ALU.mult)
+            for a in range(2):
+                nc.vector.tensor_tensor(packed(gain[:, a, :]), split(inp, a), pairs(slope[t], a), ALU.mult)
+                add_pairs(inp, a, False)
+            for a in range(2):
+                nc.vector.scalar_tensor_tensor(split(low, a), pairs(cost[t][:], a), 0.36 / 0.64, packed(gain[:, a, :]), ALU.mult, ALU.min)
+                add_pairs(low, a, a == 1)
 
         def finish(t):
             for h in range(2):
@@ -233,8 +253,11 @@ def tile_picked_ydbtune_rel_p_kernel(
                     ALU.mult,
                     ALU.mult,
                 )
-            for u in range(2):
-                nc.scalar.activation(planes[u][:, t, :], ratio_w[t][:].indirect(wl_sb[:, u * UH // 16 : (u + 1) * UH // 16]), ACT.Copy)
+            if t < TILES - 1:
+                nc.scalar.activation(planes[:, t, :], ratio_w[t][:].indirect(wl_sb[:]), ACT.Copy)
+            else:
+                for u, (a, b) in enumerate(PIECES):
+                    nc.scalar.activation(last_plane[u][:], ratio_w[t][:].indirect(wl_sb[:, a // 16 : b // 16]), ACT.Copy)
 
         gather_child(2)
         gather_child(3)
@@ -242,31 +265,29 @@ def tile_picked_ydbtune_rel_p_kernel(
             join_costs(t)
             if t >= 1:
                 finish(t - 1)
+        for u, (a, b) in enumerate(PIECES):
+            nc.vector.tensor_copy(hid[u][:, :, : TILES - 1], planes[:, :, a:b].rearrange("p t c -> p c t"))
         finish(TILES - 1)
 
-        for u in range(2):
-            hid = ring.tile([P, UH, TILES], BF16, name="hid", align_bytes=64)
-            nc.vector.tensor_copy(
-                hid[:].rearrange("p (c i) t -> p c t i", i=4),
-                planes[u][:].rearrange("p t (c i) -> p c t i", i=4),
-            )
-            hid_words = ring.tile([P, UH], U32, name="hid_words", align_bytes=64)
-            hid_scales = ring.tile([P, UH], U8, name="hid_scales", align_bytes=64)
-            nc.vector.quantize_mx(out=hid_words[:].bitcast(FP8X4), scales=hid_scales[:], in_=hid[:].rearrange("p c t -> p (c t)"))
+        for u, (a, b) in enumerate(PIECES):
+            nc.vector.tensor_copy(hid[u][:, :, TILES - 1], last_plane[u][:])
+            hid_words = keep.tile([P, b - a], U32, name=f"hid_words{u}", align_bytes=64)
+            hid_scales = keep.tile([P, b - a], U8, name=f"hid_scales{u}", align_bytes=64)
+            nc.vector.quantize_mx(out=hid_words[:].bitcast(FP8X4), scales=hid_scales[:], in_=hid[u][:].rearrange("p c t -> p (c t)"))
             for mb in range(N // P):
-                acc = bank(u, mb, UH, f"knobs{u}{mb}")
+                acc = bank(u, mb, b - a, f"knobs{u}{mb}")
                 nc.tensor.matmul_mx(
                     out=acc[:],
-                    lhsT=w_raw[:, 2 * P * mb : 2 * P * (mb + 1)].bitcast(FP4X4),
+                    lhsT=w3_sb[:, 2 * P * mb : 2 * P * (mb + 1)].bitcast(FP4X4),
                     lhsT_scale=ws_raw[:, P * mb : P * (mb + 1)],
                     rhs=hid_words[:].bitcast(FP8X4),
                     rhs_scale=hid_scales[:],
                     start=True,
                     stop=True,
                 )
-                result = keep.tile([P, UH], F32, name=f"result{u}{mb}")
+                result = keep.tile([P, b - a], F32, name=f"result{u}{mb}")
                 if mb == 0:
                     nc.scalar.copy(result[:], acc[:])
                 else:
                     nc.vector.tensor_copy(result[:], acc[:])
-                (nc.scalar if mb == 0 else nc.sync).dma_start(out=out[P * mb : P * (mb + 1), u * UH : (u + 1) * UH], in_=result[:])
+                (nc.scalar if mb == 0 else nc.sync).dma_start(out=out[P * mb : P * (mb + 1), a:b], in_=result[:])

@@ -119,8 +119,7 @@ def tile_picked_ydbtune_rel_p_kernel(
         tanh_w[2] = head.tile([P, 2 * S], F32, name="tanh_w2", align_bytes=64, offset=2 * T)
         tanh_w[3] = head.tile([P, 2 * S], F32, name="tanh_w3", align_bytes=64, offset=4 * T)
 
-        def product(i, t, h, name):
-            acc = bank(t, h, HALF, name)
+        def product(i, t, h, acc):
             nc.tensor.matmul_mx(
                 out=acc[:],
                 lhsT=w_dealt[i][:, 2 * P * t : 2 * P * (t + 1)].bitcast(FP4X4),
@@ -135,15 +134,20 @@ def tile_picked_ydbtune_rel_p_kernel(
         def chd_half(h):
             return chd_sb[:, h * HALF // 16 : (h + 1) * HALF // 16]
 
-        for t in range(TILES):
+        def selectivity(t, banks):
             for h in range(2):
-                se = product(0, t, h, f"se{t}{h}")
+                se = product(0, t, h, bank(*banks[h], HALF, f"se{t}{h}"))
                 nc.scalar.activation(tanh_w[t][:, half(h)], se[:], ACT.Tanh, scale=0.5)
 
-        w3_sb = keep.tile([P, 2 * N], U8, name="w3_sb", tag="w2_dealt", align_bytes=64)
-        nc.sync.dma_start(out=w3_sb[:].bitcast(I32), in_=w3_words[0].bitcast(I32))
+        for t in range(TILES):
+            selectivity(t, ((t, 0), (t, 1)))
 
-        slope = [tanh_w[2][:, S:], tanh_w[3][:, S:]] + [keep.tile([P, S], F32, name=f"slope{t}")[:] for t in (2, 3)]
+        slope = [
+            tanh_w[2][:, S:],
+            tanh_w[3][:, S:],
+            keep.tile([P, S], F32, name="slope2")[:],
+            keep.tile([P, S], F32, name="slope3")[:],
+        ]
 
         def gather_slope(t):
             for h in range(2):
@@ -155,29 +159,34 @@ def tile_picked_ydbtune_rel_p_kernel(
         expo = [keep.tile([P, S], F32, name=f"expo{t}", tag=f"expo{t}") for t in range(TILES)]
         for t in range(TILES):
             for h in range(2):
-                cs[t, h] = product(1, t, h, f"cs{t}{h}")
+                cs[t, h] = product(1, t, h, bank(t, h, HALF, f"cs{t}{h}"))
                 nc.scalar.activation(expo[t][:, half(h)], cs[t, h][:], ACT.Exp)
         gather_slope(2)
         gather_slope(3)
 
-        cost = [keep.tile([P, S], F32, name=f"cost{t}") for t in range(TILES)]
+        cost = [keep.tile([P, S], F32, name=f"cost{t}", tag=f"cost{t}") for t in range(TILES)]
         ratio_w = [keep.tile([P, S], F32, name=f"ratio_w{t}") for t in range(TILES)]
-        log_den = keep.tile([P, TILES * V], F32, name="log_den")
+        log_den = keep.tile([P, TILES * V], F32, name="log_den", tag="log_den")
         inv_den = keep.tile([P, TILES * V], F32, name="inv_den")
         sums = {}
 
-        def add_groups(t, h, src_of_d, first, last):
-            for d in range(D):
-                nc.tensor.matmul(sums[t, h][:], src_of_d(d), ident[:], is_transpose=True, start=first and d == 0, stop=last and d == D - 1)
-
         def softplus(t):
             soft = keep.tile([P, S], F32, name=f"soft{t}")
-            nc.scalar.activation(soft[:], expo[t][:], ACT.Ln, bias=1.0)
+            for cols in (half(0), half(1)) if t == 0 else (slice(0, S),):
+                nc.scalar.activation(soft[:, cols], expo[t][:, cols], ACT.Ln, bias=1.0)
             for h in range(2):
                 nc.vector.scalar_tensor_tensor(cost[t][:, half(h)], soft[:, half(h)], LN_CAP, cs[t, h][:], ALU.min, ALU.max)
+            sums[t] = bank(t, 0, V, f"sums{t}")
             for h in range(2):
-                sums[t, h] = bank(t, h, P, f"sums{t}{h}")
-                add_groups(t, h, lambda d: cost[t][:, h * HALF + d : (h + 1) * HALF : D], True, False)
+                for d in range(D):
+                    nc.tensor.matmul(
+                        sums[t][:, h * VH : (h + 1) * VH],
+                        cost[t][:, h * HALF + d : (h + 1) * HALF : D],
+                        ident[:],
+                        is_transpose=True,
+                        start=h == 0 and d == 0,
+                        stop=False,
+                    )
 
         def largest(ts):
             for t in ts:
@@ -199,14 +208,17 @@ def tile_picked_ydbtune_rel_p_kernel(
         softplus(2)
         softplus(3)
         largest((2, 3))
-        gather_child(0)
-        gather_child(1)
+        for t in range(TILES):
+            gather_child(t)
         for t in range(TILES):
             nc.scalar.activation(log_den[:, V * t : V * (t + 1)], ratio_w[t][:, V : 2 * V], ACT.Ln, bias=0.5)
         nc.scalar.activation(inv_den[:], log_den[:], ACT.Exp, scale=-1.0)
 
-        planes = keep.tile([P, TILES - 1, U], BF16, name="planes")
-        last_plane = [keep.tile([P, b - a], BF16, name=f"last_plane{a}") for a, b in PIECES]
+        w3_sb = keep.tile([P, 2 * N], U8, name="w3_sb", tag="w2_dealt", align_bytes=64)
+        nc.sync.dma_start(out=w3_sb[:].bitcast(I32), in_=w3_words[0].bitcast(I32))
+
+        early_planes = keep.tile([P, 2, U], BF16, name="early_planes")
+        late_planes = [keep.tile([P, 2, b - a], BF16, name=f"late_planes{a}") for a, b in PIECES]
         hid = [keep.tile([P, b - a, TILES], BF16, name=f"hid{a}", align_bytes=64) for a, b in PIECES]
 
         def join_costs(t):
@@ -227,7 +239,7 @@ def tile_picked_ydbtune_rel_p_kernel(
                 for h in range(2):
                     for b in range(2):
                         nc.tensor.matmul(
-                            sums[t, h][:], src[:, 2 * a + b, VH * h : VH * (h + 1)], ident[:], is_transpose=True, start=False, stop=last and b == 1
+                            sums[t][:, VH * h : VH * (h + 1)], src[:, 2 * a + b, VH * h : VH * (h + 1)], ident[:], is_transpose=True, start=False, stop=last and h == 1 and b == 1
                         )
 
             for a in range(2):
@@ -239,38 +251,34 @@ def tile_picked_ydbtune_rel_p_kernel(
                 nc.vector.scalar_tensor_tensor(split(low, a), pairs(cost[t][:], a), 0.36 / 0.64, packed(gain[:, a, :]), ALU.mult, ALU.min)
                 add_pairs(low, a, a == 1)
 
-        def finish(t):
+        def settle(t):
+            turned = keep.tile([P, V], F32, name=f"turned{t}", tag="cost2")
+            nc.scalar.copy(turned[:], sums[t][:])
+            plan = bank(t, 1, V, f"plan{t}")
             for h in range(2):
-                turned = ring.tile([P, P], F32, name="turned")
-                nc.scalar.copy(turned[:], sums[t, h][:])
-                plan = bank(t, h, P, f"plan{t}{h}")
-                nc.tensor.transpose(plan[:], turned[:], ident[:])
-                nc.vector.scalar_tensor_tensor(
-                    ratio_w[t][:, h * VH : (h + 1) * VH],
-                    plan[:],
-                    unit64[:, t : t + 1],
-                    inv_den[:, V * t + h * VH : V * t + (h + 1) * VH],
-                    ALU.mult,
-                    ALU.mult,
-                )
-            if t < TILES - 1:
-                nc.scalar.activation(planes[:, t, :], ratio_w[t][:].indirect(wl_sb[:]), ACT.Copy)
-            else:
-                for u, (a, b) in enumerate(PIECES):
-                    nc.scalar.activation(last_plane[u][:], ratio_w[t][:].indirect(wl_sb[:, a // 16 : b // 16]), ACT.Copy)
+                nc.tensor.transpose(plan[:, h * VH : (h + 1) * VH], turned[:, h * VH : (h + 1) * VH], ident[:])
+            nc.vector.scalar_tensor_tensor(ratio_w[t][:, :V], plan[:], unit64[:, t : t + 1], inv_den[:, V * t : V * (t + 1)], ALU.mult, ALU.mult)
 
-        gather_child(2)
-        gather_child(3)
-        for t in range(TILES):
-            join_costs(t)
-            if t >= 1:
-                finish(t - 1)
+        def slots(a, b):
+            return wl_sb[:, a // 16 : b // 16]
+
+        join_costs(0)
+        join_costs(1)
+        join_costs(2)
+        for t in range(3):
+            settle(t)
+        for t in range(2):
+            nc.scalar.activation(early_planes[:, t, :], ratio_w[t][:].indirect(wl_sb[:]), ACT.Copy)
+        join_costs(3)
         for u, (a, b) in enumerate(PIECES):
-            nc.vector.tensor_copy(hid[u][:, :, : TILES - 1], planes[:, :, a:b].rearrange("p t c -> p c t"))
-        finish(TILES - 1)
+            nc.scalar.activation(late_planes[u][:, 0, :], ratio_w[2][:].indirect(slots(a, b)), ACT.Copy)
+        settle(3)
+        for u, (a, b) in enumerate(PIECES):
+            nc.vector.tensor_copy(hid[u][:, :, 0:2], early_planes[:, :, a:b].rearrange("p t c -> p c t"))
 
         for u, (a, b) in enumerate(PIECES):
-            nc.vector.tensor_copy(hid[u][:, :, TILES - 1], last_plane[u][:])
+            nc.scalar.activation(late_planes[u][:, 1, :], ratio_w[3][:].indirect(slots(a, b)), ACT.Copy)
+            nc.vector.tensor_copy(hid[u][:, :, 2:4], late_planes[u][:].rearrange("p t c -> p c t"))
             hid_words = keep.tile([P, b - a], U32, name=f"hid_words{u}", align_bytes=64)
             hid_scales = keep.tile([P, b - a], U8, name=f"hid_scales{u}", align_bytes=64)
             nc.vector.quantize_mx(out=hid_words[:].bitcast(FP8X4), scales=hid_scales[:], in_=hid[u][:].rearrange("p c t -> p (c t)"))

@@ -222,34 +222,30 @@ def tile_picked_ydbtune_rel_p_kernel(
         hid = [keep.tile([P, b - a, TILES], BF16, name=f"hid{a}", align_bytes=64) for a, b in PIECES]
 
         def join_costs(t):
-            inp = ring.tile([P, D, V], F32, name="inp")
-            gain = ring.tile([P, 2, HALF], F32, name="gain")
-            low = ring.tile([P, D, V], F32, name="low")
-
-            def pairs(row, a):
-                return row.rearrange("p (v d) -> p v d", d=D)[:, :, 2 * a : 2 * a + 2]
-
-            def packed(plane):
-                return plane.rearrange("p (v b) -> p v b", b=2)
-
-            def split(planes_by_d, a):
-                return planes_by_d[:, 2 * a : 2 * a + 2, :].rearrange("p b v -> p v b")
-
-            def add_pairs(src, a, last):
-                for h in range(2):
-                    for b in range(2):
-                        nc.tensor.matmul(
-                            sums[t][:, VH * h : VH * (h + 1)], src[:, 2 * a + b, VH * h : VH * (h + 1)], ident[:], is_transpose=True, start=False, stop=last and h == 1 and b == 1
-                        )
-
-            for a in range(2):
-                nc.vector.scalar_tensor_tensor(split(inp, a), pairs(tanh_w[t][:, :S], a), 1.0, pairs(child[t][:], a), ALU.add, ALU.mult)
-            for a in range(2):
-                nc.vector.tensor_tensor(packed(gain[:, a, :]), split(inp, a), pairs(slope[t], a), ALU.mult)
-                add_pairs(inp, a, False)
-            for a in range(2):
-                nc.vector.scalar_tensor_tensor(split(low, a), pairs(cost[t][:], a), 0.36 / 0.64, packed(gain[:, a, :]), ALU.mult, ALU.min)
-                add_pairs(low, a, a == 1)
+            inp = ring.tile([P, S], F32, name="inp")
+            gain = ring.tile([P, S], F32, name="gain")
+            low = ring.tile([P, 2, D, VH], F32, name="low")
+            for h in range(2):
+                nc.vector.scalar_tensor_tensor(inp[:, half(h)], tanh_w[t][:, half(h)], 1.0, child[t][:, half(h)], ALU.add, ALU.mult)
+            for h in range(2):
+                nc.vector.tensor_tensor(gain[:, half(h)], inp[:, half(h)], slope[t][:, half(h)], ALU.mult)
+                for d in range(D):
+                    nc.tensor.matmul(
+                        sums[t][:, VH * h : VH * (h + 1)], inp[:, h * HALF + d : (h + 1) * HALF : D], ident[:], is_transpose=True, start=False, stop=False
+                    )
+            for h in range(2):
+                nc.vector.scalar_tensor_tensor(
+                    low[:, h].rearrange("p d v -> p v d"),
+                    cost[t][:, half(h)].rearrange("p (v d) -> p v d", d=D),
+                    0.36 / 0.64,
+                    gain[:, half(h)].rearrange("p (v d) -> p v d", d=D),
+                    ALU.mult,
+                    ALU.min,
+                )
+                for d in range(D):
+                    nc.tensor.matmul(
+                        sums[t][:, VH * h : VH * (h + 1)], low[:, h, d, :], ident[:], is_transpose=True, start=False, stop=h == 1 and d == D - 1
+                    )
 
         def settle(t):
             turned = keep.tile([P, V], F32, name=f"turned{t}", tag="cost2")

from contextlib import ExitStack

import concourse.mybir as mybir
from concourse.masks import make_identity

K, T, S, D, N, H, V, U = 512, 4096, 1024, 4, 256, 512, 256, 512
FLOPS = 2 * K * H * S * 2 + 2 * H * N * U

F32 = mybir.dt.float32
BF16 = mybir.dt.bfloat16
I32 = mybir.dt.int32
U32 = mybir.dt.uint32
U16 = mybir.dt.uint16
U8 = mybir.dt.uint8
FP8X4 = mybir.dt.float8_e4m3fn_x4
FP4X4 = mybir.dt.float4_e2m1fn_x4
ACT = mybir.ActivationFunctionType
ALU = mybir.AluOpType

P = 128
TILES = H // P
HALF = S // 2
VH = V // 2
PIECES = ((0, 256), (256, 512))
LN_CAP = 44.0


def tile_picked_ydbtune_rel_p_kernel(
    tc, x_words, x_scales, w1_words, w1_scales, w2_words, w2_scales, unit, w3_words, w3_scales, offs, chd, wl, out
):
    nc = tc.nc
    with ExitStack() as ctx:
        keep = ctx.enter_context(tc.tile_pool(name="keep", bufs=1))
        head = ctx.enter_context(tc.tile_pool(name="head", bufs=1))
        ring = ctx.enter_context(tc.tile_pool(name="ring", bufs=2))
        psum = ctx.enter_context(tc.psum_pool(name="psum", bufs=1))

        def bank(t, h, cols, name):
            return psum.tile([P, cols], F32, tag=f"bank{2 * t + h}", name=name)

        def half(h):
            return slice(h * HALF, (h + 1) * HALF)

        def load_scale_rows(queue, dst, src):
            for q in range(4):
                queue.dma_start(out=dst[32 * q : 32 * q + 4, :].bitcast(I32), in_=src[0, 4 * q : 4 * q + 4, :].bitcast(I32))

        offs_sb = keep.tile([P, S // 16], U16, name="offs_sb")
        chd_sb = keep.tile([P, S // 16], U16, name="chd_sb")
        wl_sb = keep.tile([P, U // 16], U16, name="wl_sb")
        x_table = keep.tile([P, T], U32, name="x_table", tag="x_table", align_bytes=64)
        xs_table = head.tile([P, T], U8, name="xs_table", align_bytes=64, offset=0)
        w_raw = keep.tile([P, 2 * H], U8, name="w_raw", tag="w_raw", align_bytes=64)
        ws_raw = keep.tile([P, H], U8, name="ws_raw", align_bytes=64)
        unit_sb = keep.tile([P, TILES], F32, name="unit_sb")
        w1_staged = head.tile([P, 3 * H], U8, name="w1_staged", align_bytes=64, offset=4 * T - 2 * H)
        w1_raw = w1_staged[:, : 2 * H]
        w1s_raw = w1_staged[:, 2 * H :]
        tanh_w = {t: keep.tile([P, 2 * S], F32, name=f"tanh_w{t}") for t in (0, 1)}

        nc.vector.memset(xs_table[:].bitcast(I32), 0)
        nc.gpsimd.memset(ws_raw[:].bitcast(I32), 0)
        nc.gpsimd.memset(w1s_raw.bitcast(I32), 0)

        x_rows = x_words[0].rearrange("p n t -> p (n t)").bitcast(I32)
        nc.sync.dma_start(offs_sb[:], offs)
        nc.scalar.dma_start(out=w_raw[:].bitcast(I32), in_=w2_words[0].bitcast(I32))
        nc.sync.dma_start(out=x_table[:, : T // 4].bitcast(I32), in_=x_rows[:, : T // 4])
        load_scale_rows(nc.sync, xs_table, x_scales)
        nc.sync.dma_start(out=x_table[:, T // 4 :].bitcast(I32), in_=x_rows[:, T // 4 :])
        load_scale_rows(nc.gpsimd, ws_raw, w2_scales)
        nc.gpsimd.dma_start(out=unit_sb[:], in_=unit.rearrange("(p t) o -> p (t o)", t=TILES))
        nc.sync.dma_start(chd_sb[:], chd)
        nc.sync.dma_start(wl_sb[:], wl)
        nc.sync.dma_start(out=w1_raw.bitcast(I32), in_=w1_words[0].bitcast(I32))
        load_scale_rows(nc.sync, w1s_raw, w1_scales)

        for t in range(2):
            nc.vector.memset(tanh_w[t][:, S:], 0.0)
        ident = keep.tile([P, P], F32, name="ident")
        make_identity(nc, ident[:])

        unit64 = keep.tile([P, TILES], F32, name="unit64")
        nc.scalar.activation(unit64[:], unit_sb[:], ACT.Copy, scale=0.64)

        w_dealt = {}
        ws_dealt = {}

        def deal_words(i, words, raw):
            w_dealt[i] = words
            nc.vector.tensor_copy(
                words.rearrange("p (t m b) -> p t m b", t=TILES, b=2),
                raw.rearrange("p (m t b) -> p t m b", t=TILES, b=2),
            )

        def deal_scales(i, scales, raw):
            ws_dealt[i] = scales
            nc.vector.tensor_copy(
                scales.rearrange("p (t m) -> p t m", t=TILES),
                raw.rearrange("p (m t) -> p t m", t=TILES),
            )

        w2_dealt = keep.tile([P, 2 * H], U8, name="w2_dealt", tag="w2_dealt", align_bytes=64)
        deal_words(0, w2_dealt[:], w_raw[:])
        xq_scales = keep.tile([P, S], U8, name="xq_scales", tag="w_raw", align_bytes=64)
        nc.vector.tensor_copy(xq_scales[:], xs_table[:].indirect(offs_sb[:]))
        xq_words = [
            head.tile([P, HALF], U32, name="xq_words0", align_bytes=64, offset=0),
            head.tile([P, HALF], U32, name="xq_words1", align_bytes=64, offset=4 * HALF + H),
        ]
        w2s_dealt = head.tile([P, H], U8, name="w2s_dealt", align_bytes=64, offset=4 * HALF)
        deal_scales(0, w2s_dealt[:], ws_raw[:])
        load_scale_rows(nc.sync, ws_raw[:, :N], w3_scales)
        for h in range(2):
            nc.vector.tensor_copy(xq_words[h][:], x_table[:].indirect(offs_sb[:, h * HALF // 16 : (h + 1) * HALF // 16]))
        w1_dealt = keep.tile([P, 3 * H], U8, name="w1_dealt", tag="x_table", align_bytes=64)
        deal_words(1, w1_dealt[:, : 2 * H], w1_raw)
        deal_scales(1, w1_dealt[:, 2 * H :], w1s_raw)
        tanh_w[2] = head.tile([P, 2 * S], F32, name="tanh_w2", align_bytes=64, offset=2 * T)
        tanh_w[3] = head.tile([P, 2 * S], F32, name="tanh_w3", align_bytes=64, offset=4 * T)

        def product(i, t, h, acc):
            nc.tensor.matmul_mx(
                out=acc[:],
                lhsT=w_dealt[i][:, 2 * P * t : 2 * P * (t + 1)].bitcast(FP4X4),
                lhsT_scale=ws_dealt[i][:, P * t : P * (t + 1)],
                rhs=xq_words[h][:].bitcast(FP8X4),
                rhs_scale=xq_scales[:, half(h)],
                start=True,
                stop=True,
            )
            return acc

        def chd_half(h):
            return chd_sb[:, h * HALF // 16 : (h + 1) * HALF // 16]

        def selectivity(t, banks):
            for h in range(2):
                se = product(0, t, h, bank(*banks[h], HALF, f"se{t}{h}"))
                nc.scalar.activation(tanh_w[t][:, half(h)], se[:], ACT.Tanh, scale=0.5)

        for t in range(TILES):
            selectivity(t, ((t, 0), (t, 1)))

        slope = [
            tanh_w[2][:, S:],
            tanh_w[3][:, S:],
            keep.tile([P, S], F32, name="slope2")[:],
            keep.tile([P, S], F32, name="slope3")[:],
        ]

        def gather_slope(t):
            for h in range(2):
                nc.vector.tensor_scalar(slope[t][:, half(h)], tanh_w[t][:].indirect(chd_half(h)), 0.8, 0.28, ALU.mult, ALU.add)

        gather_slope(0)
        gather_slope(1)
        cs = {}
        expo = [keep.tile([P, S], F32, name=f"expo{t}", tag=f"expo{t}") for t in range(TILES)]
        for t in range(TILES):
            for h in range(2):
                cs[t, h] = product(1, t, h, bank(t, h, HALF, f"cs{t}{h}"))
                nc.scalar.activation(expo[t][:, half(h)], cs[t, h][:], ACT.Exp)
        gather_slope(2)
        gather_slope(3)

        cost = [keep.tile([P, S], F32, name=f"cost{t}", tag=f"cost{t}") for t in range(TILES)]
        ratio_w = [keep.tile([P, S], F32, name=f"ratio_w{t}") for t in range(TILES)]
        log_den = keep.tile([P, TILES * V], F32, name="log_den", tag="log_den")
        inv_den = keep.tile([P, TILES * V], F32, name="inv_den")
        sums = {}

        def softplus(t):
            soft = keep.tile([P, S], F32, name=f"soft{t}")
            for cols in (half(0), half(1)) if t == 0 else (slice(0, S),):
                nc.scalar.activation(soft[:, cols], expo[t][:, cols], ACT.Ln, bias=1.0)
            for h in range(2):
                nc.vector.scalar_tensor_tensor(cost[t][:, half(h)], soft[:, half(h)], LN_CAP, cs[t, h][:], ALU.min, ALU.max)
            sums[t] = bank(t, 0, V, f"sums{t}")
            for h in range(2):
                for d in range(D):
                    nc.tensor.matmul(
                        sums[t][:, h * VH : (h + 1) * VH],
                        cost[t][:, h * HALF + d : (h + 1) * HALF : D],
                        ident[:],
                        is_transpose=True,
                        start=h == 0 and d == 0,
                        stop=False,
                    )

        def largest(ts):
            for t in ts:
                quad = cost[t][:].rearrange("p (v d) -> p v d", d=D)
                nc.vector.tensor_tensor(ratio_w[t][:, 2 * V :].rearrange("p (v e) -> p v e", e=2), quad[:, :, 0:2], quad[:, :, 2:4], ALU.max)
            for t in ts:
                nc.vector.tensor_tensor(ratio_w[t][:, V : 2 * V], ratio_w[t][:, 2 * V :: 2], ratio_w[t][:, 2 * V + 1 :: 2], ALU.max)

        child = {}

        def gather_child(t):
            child[t] = keep.tile([P, S], F32, name=f"child{t}", tag=f"expo{t}")
            for h in range(2):
                nc.scalar.activation(child[t][:, half(h)], cost[t][:].indirect(chd_half(h)), ACT.Copy, scale=0.5 / 0.64)

        softplus(0)
        softplus(1)
        largest((0, 1))
        softplus(2)
        softplus(3)
        largest((2, 3))
        for t in range(TILES):
            gather_child(t)
        for t in range(TILES):
            nc.scalar.activation(log_den[:, V * t : V * (t + 1)], ratio_w[t][:, V : 2 * V], ACT.Ln, bias=0.5)
        nc.scalar.activation(inv_den[:], log_den[:], ACT.Exp, scale=-1.0)

        w3_sb = keep.tile([P, 2 * N], U8, name="w3_sb", tag="w2_dealt", align_bytes=64)
        nc.sync.dma_start(out=w3_sb[:].bitcast(I32), in_=w3_words[0].bitcast(I32))

        early_planes = keep.tile([P, 2, U], BF16, name="early_planes")
        late_planes = [keep.tile([P, 2, b - a], BF16, name=f"late_planes{a}") for a, b in PIECES]
        hid = [keep.tile([P, b - a, TILES], BF16, name=f"hid{a}", align_bytes=64) for a, b in PIECES]

        def join_costs(t):
            inp = ring.tile([P, S], F32, name="inp")
            gain = ring.tile([P, S], F32, name="gain")
            low = ring.tile([P, 2, D, VH], F32, name="low")
            for h in range(2):
                nc.vector.scalar_tensor_tensor(inp[:, half(h)], tanh_w[t][:, half(h)], 1.0, child[t][:, half(h)], ALU.add, ALU.mult)
            for h in range(2):
                nc.vector.tensor_tensor(gain[:, half(h)], inp[:, half(h)], slope[t][:, half(h)], ALU.mult)
                for d in range(D):
                    nc.tensor.matmul(
                        sums[t][:, VH * h : VH * (h + 1)], inp[:, h * HALF + d : (h + 1) * HALF : D], ident[:], is_transpose=True, start=False, stop=False
                    )
            for h in range(2):
                nc.vector.scalar_tensor_tensor(
                    low[:, h].rearrange("p d v -> p v d"),
                    cost[t][:, half(h)].rearrange("p (v d) -> p v d", d=D),
                    0.36 / 0.64,
                    gain[:, half(h)].rearrange("p (v d) -> p v d", d=D),
                    ALU.mult,
                    ALU.min,
                )
                for d in range(D):
                    nc.tensor.matmul(
                        sums[t][:, VH * h : VH * (h + 1)], low[:, h, d, :], ident[:], is_transpose=True, start=False, stop=h == 1 and d == D - 1
                    )

        def settle(t):
            turned = keep.tile([P, V], F32, name=f"turned{t}", tag="cost2")
            nc.scalar.copy(turned[:], sums[t][:])
            plan = bank(t, 1, V, f"plan{t}")
            for h in range(2):
                nc.tensor.transpose(plan[:, h * VH : (h + 1) * VH], turned[:, h * VH : (h + 1) * VH], ident[:])
            nc.vector.scalar_tensor_tensor(ratio_w[t][:, :V], plan[:], unit64[:, t : t + 1], inv_den[:, V * t : V * (t + 1)], ALU.mult, ALU.mult)

        def slots(a, b):
            return wl_sb[:, a // 16 : b // 16]

        join_costs(0)
        join_costs(1)
        join_costs(2)
        for t in range(3):
            settle(t)
        for t in range(2):
            nc.scalar.activation(early_planes[:, t, :], ratio_w[t][:].indirect(wl_sb[:]), ACT.Copy)
        join_costs(3)
        for u, (a, b) in enumerate(PIECES):
            nc.scalar.activation(late_planes[u][:, 0, :], ratio_w[2][:].indirect(slots(a, b)), ACT.Copy)
        settle(3)
        for u, (a, b) in enumerate(PIECES):
            nc.vector.tensor_copy(hid[u][:, :, 0:2], early_planes[:, :, a:b].rearrange("p t c -> p c t"))

        for u, (a, b) in enumerate(PIECES):
            nc.scalar.activation(late_planes[u][:, 1, :], ratio_w[3][:].indirect(slots(a, b)), ACT.Copy)
            nc.vector.tensor_copy(hid[u][:, :, 2:4], late_planes[u][:].rearrange("p t c -> p c t"))
            hid_words = keep.tile([P, b - a], U32, name=f"hid_words{u}", align_bytes=64)
            hid_scales = keep.tile([P, b - a], U8, name=f"hid_scales{u}", align_bytes=64)
            nc.vector.quantize_mx(out=hid_words[:].bitcast(FP8X4), scales=hid_scales[:], in_=hid[u][:].rearrange("p c t -> p (c t)"))
            for mb in range(N // P):
                acc = bank(u, mb, b - a, f"knobs{u}{mb}")
                nc.tensor.matmul_mx(
                    out=acc[:],
                    lhsT=w3_sb[:, 2 * P * mb : 2 * P * (mb + 1)].bitcast(FP4X4),
                    lhsT_scale=ws_raw[:, P * mb : P * (mb + 1)],
                    rhs=hid_words[:].bitcast(FP8X4),
                    rhs_scale=hid_scales[:],
                    start=True,
                    stop=True,
                )
                result = keep.tile([P, b - a], F32, name=f"result{u}{mb}")
                if mb == 0:
                    nc.scalar.copy(result[:], acc[:])
                else:
                    nc.vector.tensor_copy(result[:], acc[:])
                (nc.scalar if mb == 0 else nc.sync).dma_start(out=out[P * mb : P * (mb + 1), a:b], in_=result[:])
